import numpy as np, ml_dtypes
CORES = [4,5,6,7,0,1,2,3]
N = 8
ROOT = 0
def setup_inputs(rng):
    return {"x": rng.standard_normal((N, 128, 8), dtype=np.float32).astype(ml_dtypes.bfloat16)}
def reference(x):
    y = np.full((N, 128, N * 8), np.nan, x.dtype)
    y[ROOT] = np.concatenate(list(x), axis=1)
    return {"y": y}

W = 8
N = 8

SCRATCH = {
    "land": ("sbuf", [128, N * W], "bfloat16"),
}
SEMAPHORES = ["loaded", "read", "arrived", "stored"]


def engines(mask):
    return bin(mask).count("1")


def rank_program(g, core, T, topo):
    rank = T.rank_of(core)
    if rank is None:
        return
    root = T.cores[T.root if T.root is not None else 0]
    block = T.land[:, rank * W:(rank + 1) * W]

    g.dma_start(block, T.x[:]).then_inc(T.sem.loaded, 16)
    g.wait_ge(T.sem.loaded, 16)

    if core != root:
        rid, pid = topo.addr(root)[0:2]
        mask = topo.mask(core, root)
        g.remote_dma(block, block, T.sem.arrived, T.sem.read, pid, rid, mask)
        g.wait_ge(T.sem.read, engines(mask))
        return

    total = sum(engines(topo.mask(c, root)) for c in T.cores if c != root)
    g.wait_ge(T.sem.arrived, total)
    g.dma_start(T.y[:], T.land[:]).then_inc(T.sem.stored, 16)
    g.wait_ge(T.sem.stored, 16)
